import numpy as np
import ml_dtypes


def mxq(x, axis, fmt="e4m3"):
    dtype, down = {"e4m3": (ml_dtypes.float8_e4m3fn, 7), "e5m2": (ml_dtypes.float8_e5m2, 14)}[fmt]
    v = np.moveaxis(np.asarray(x, np.float32).astype(ml_dtypes.bfloat16).astype(np.float64), axis, -1)
    blocks = v.reshape(v.shape[:-1] + (-1, 32))
    amax = np.abs(blocks).max(-1, keepdims=True)
    byte = np.maximum(np.where(amax > 0, np.frexp(amax)[1] - 1 + 127, 0) - down, 1)
    scale = np.exp2(byte - 127.0)
    codes = (blocks / scale).astype(np.float32).astype(dtype).astype(np.float64)
    return np.moveaxis((codes * scale).reshape(v.shape), -1, axis)


WIDE = False


def mx_kscale(k):
    if not WIDE:
        return np.ones(k)
    levels = np.array([10, -10, 5, -5, 0])
    if k % 512:
        return np.exp2(np.random.permutation(np.resize(levels, k // 32))).repeat(32)
    a = np.empty((k // 512, 16))
    for p in range(k // 512):
        a[p, :8] = np.random.permutation(np.resize(levels, 8))
        for g in range(8):
            far = levels[np.abs(levels - a[p, g]) >= 10]
            a[p, g + 8] = far[np.random.randint(len(far))]
    return np.exp2(a.ravel()).repeat(32)


def f64(x):
    return np.asarray(x).astype(np.float64)


def striped(idx):
    return np.tile(np.asarray(idx).reshape(-1, 16).T, (8, 1)).astype(np.uint16)


def unstriped(offs):
    return offs[:16].T.reshape(-1).astype(np.int64)


E2M1 = np.array([0.0, 0.5, 1.0, 1.5, 2.0, 3.0, 4.0, 6.0, -0.0, -0.5, -1.0, -1.5, -2.0, -3.0, -4.0, -6.0])


def pack_weight(w, fmt):
    k, n = w.shape
    w = f64(np.asarray(w, np.float32).astype(ml_dtypes.bfloat16)).reshape(k // 32, 32, n)
    amax = np.abs(w).max(1)
    if fmt == "e4m3":
        byte = np.frexp(amax)[1] - 1 + 127 - 7
    else:
        mant, ex = np.frexp(amax / 6.0)
        byte = np.where(mant > 0.5, ex, ex - 1) + 127
    byte = np.clip(np.where(amax > 0, byte, 1), 1, 254)
    scaled = (w * np.exp2(127.0 - byte)[:, None, :]).reshape(k, n).astype(np.float32)
    by_word = np.ascontiguousarray(scaled.reshape(k // 512, 128, 4, n).transpose(0, 1, 3, 2))
    if fmt == "e4m3":
        words = by_word.astype(ml_dtypes.float8_e4m3fn).view(np.uint8)
    else:
        c = by_word.astype(ml_dtypes.float4_e2m1fn).view(np.uint8) & 0xF
        words = (c[..., 0::2] | (c[..., 1::2] << 4)).reshape(k // 512, 128, 2 * n)
    return np.ascontiguousarray(words), np.ascontiguousarray(byte.astype(np.uint8).reshape(k // 512, 16, n))


def unpack_weight(words, scales, fmt):
    g, _, n = scales.shape
    words = np.ascontiguousarray(words).reshape(g, 128, n, -1)
    if fmt == "e4m3":
        vals = words.view(ml_dtypes.float8_e4m3fn).astype(np.float64)
    else:
        nib = np.empty((g, 128, n, 4), np.uint8)
        nib[..., 0::2] = words & 0xF
        nib[..., 1::2] = words >> 4
        vals = E2M1[nib]
    vals = vals * np.repeat(np.exp2(scales.astype(np.float64) - 127.0), 8, axis=1)[..., None]
    return vals.transpose(0, 1, 3, 2).reshape(g * 512, n)


K, T, J, B, L, N = 512, 2048, 1024, 128, 512, 512


def setup_inputs():
    n = np.random.standard_normal
    idx = np.random.permutation(T)[:J]
    fk = mx_kscale(K)
    fl = mx_kscale(L)
    wap = pack_weight(n((K, N)) * 1 / np.sqrt(K) / fk[:, None], "e2m1")
    wbp = pack_weight(n((K, N)) * 1 / np.sqrt(K) / fk[:, None], "e4m3")
    gqp = pack_weight(n((L, B)) / fl[:, None], "e2m1")
    wcp = pack_weight(n((L, N)) * 1 / np.sqrt(L) * fl[:, None], "e4m3")
    return {
        "xt": (n((K, T))).astype(np.float32),
        "fa": (np.random.uniform(0.5, 2.0, (K, 1)) * fk[:, None]).astype(np.float32),
        "fb": (np.random.uniform(0.5, 2.0, (K, 1)) * fk[:, None]).astype(np.float32),
        "wa_words": wap[0],
        "wa_scales": wap[1],
        "wb_words": wbp[0],
        "wb_scales": wbp[1],
        "gq_words": gqp[0],
        "gq_scales": gqp[1],
        "wc_words": wcp[0],
        "wc_scales": wcp[1],
        "offs": striped(idx),
    }


def reference(xt, fa, fb, wa_words, wa_scales, wb_words, wb_scales, gq_words, gq_scales, wc_words, wc_scales, offs):
    idx = unstriped(offs)
    wau = unpack_weight(wa_words, wa_scales, "e2m1")
    wbu = unpack_weight(wb_words, wb_scales, "e4m3")
    gqu = unpack_weight(gq_words, gq_scales, "e2m1")
    wcu = unpack_weight(wc_words, wc_scales, "e4m3")
    u = f64(xt)[:, idx].reshape(K, B, J // B).max(axis=2) * f64(fa)
    v = f64(xt)[:, idx].reshape(K, B, J // B).mean(axis=2) * f64(fb)
    uq = mxq(u, 0, "e4m3")
    vq = mxq(v, 0, "e4m3")
    y = wau.T @ uq + wbu.T @ vq + wcu.T @ gqu
    return y

@@ -1,0 +1,140 @@
+from contextlib import ExitStack
+
+import concourse.mybir as mybir
+
+K, T, J, B, N = 512, 2048, 1024, 128, 512
+FLOPS = 3 * 2 * K * N * B
+
+F32 = mybir.dt.float32
+BF16 = mybir.dt.bfloat16
+I32 = mybir.dt.int32
+U32 = mybir.dt.uint32
+U16 = mybir.dt.uint16
+U8 = mybir.dt.uint8
+FP8X4 = mybir.dt.float8_e4m3fn_x4
+FP4X4 = mybir.dt.float4_e2m1fn_x4
+ALU = mybir.AluOpType
+COPY = mybir.ActivationFunctionType.Copy
+AXIS_X = mybir.AxisListType.X
+
+P = 128
+PACK = 4
+GROUP = 8
+LIST_ROWS = 16
+CHUNKS = (
+    (("s", 128), ("s", 384), ("s", 512)),
+    (("s", 512), ("s", 512)),
+    (("s", 512), ("s", 512)),
+    (("s", 256), ("s", 256), ("s", 256), ("s", 128), ("s", 128)),
+)
+
+
+def tile_list_group_range_pooling_kernel(
+    tc, xt, fa, fb, wa_words, wa_scales, wb_words, wb_scales, gq_words, gq_scales, wc_words, wc_scales, offs, out
+):
+    nc = tc.nc
+    with ExitStack() as ctx:
+        keep = ctx.enter_context(tc.tile_pool(name="keep", bufs=1))
+        psum = ctx.enter_context(tc.psum_pool(name="psum", bufs=1))
+
+        x_rows = xt.rearrange("(p t) c -> p t c", t=PACK)
+        x_sb = [keep.tile([P, T], F32, name="x%d" % t) for t in range(PACK)]
+        offsets = keep.tile([P, J // LIST_ROWS], U16, name="offsets")
+        fa_sb = keep.tile([P, PACK], F32, name="fa_sb")
+        fb_sb = keep.tile([P, PACK], F32, name="fb_sb")
+        fb_mean = keep.tile([P, PACK], F32, name="fb_mean")
+
+        nc.sync.dma_start(x_sb[0][:], x_rows[:, 0, :])
+        nc.scalar.dma_start(fb_sb[:], fb.rearrange("(p t) o -> p (t o)", t=PACK))
+        nc.sync.dma_start(offsets[:], offs)
+        nc.scalar.dma_start(fa_sb[:], fa.rearrange("(p t) o -> p (t o)", t=PACK))
+        for t in range(1, PACK):
+            nc.sync.dma_start(x_sb[t][:], x_rows[:, t, :])
+        nc.scalar.activation(fb_mean[:], fb_sb[:], COPY, scale=1.0 / GROUP)
+
+        wa_sb = keep.tile([P, 2 * N], U8, name="wa_sb", align_bytes=64)
+        wb_sb = keep.tile([P, N], U32, name="wb_sb", align_bytes=64)
+        wc_sb = keep.tile([P, N], U32, name="wc_sb", align_bytes=64)
+        gq_sb = keep.tile([P, 2 * B], U8, name="gq_sb", align_bytes=64)
+        nc.sync.dma_start(wc_sb[:].bitcast(I32), wc_words[0].rearrange("p n t -> p (n t)").bitcast(I32))
+        nc.sync.dma_start(wa_sb[:].bitcast(I32), wa_words[0].bitcast(I32))
+        nc.sync.dma_start(wb_sb[:].bitcast(I32), wb_words[0].rearrange("p n t -> p (n t)").bitcast(I32))
+        nc.sync.dma_start(gq_sb[:].bitcast(I32), gq_words[0].bitcast(I32))
+
+        scales = keep.tile([P, 3 * N + B], U8, name="scales", align_bytes=64)
+        nc.vector.memset(scales[:].bitcast(I32), 0)
+        wa_at, wb_at, wc_at, gq_at = 0, N, 2 * N, 3 * N
+        for at, src, width in ((wa_at, wa_scales, N), (wb_at, wb_scales, N), (wc_at, wc_scales, N), (gq_at, gq_scales, B)):
+            nc.scalar.dma_start(scales[0:16, at : at + width].bitcast(I32), src[0].bitcast(I32))
+        for q in range(1, 4):
+            nc.gpsimd.dma_start(scales[32 * q : 32 * q + 4, :].bitcast(I32), scales[4 * q : 4 * q + 4, :].bitcast(I32))
+
+        acc = [psum.tile([P, B], F32, name="acc%d" % m) for m in range(N // P)]
+        for m in range(N // P):
+            nc.tensor.matmul_mx(
+                out=acc[m][:],
+                lhsT=wc_sb[:, m * P : (m + 1) * P].bitcast(FP8X4),
+                lhsT_scale=scales[:, wc_at + m * P : wc_at + (m + 1) * P],
+                rhs=gq_sb[:].bitcast(FP4X4),
+                rhs_scale=scales[:, gq_at : gq_at + B],
+                start=True,
+                stop=False,
+            )
+
+        u_bf = keep.tile([P, B, PACK], BF16, name="u_bf", align_bytes=64)
+        v_bf = keep.tile([P, B, PACK], BF16, name="v_bf", align_bytes=64)
+        largest = keep.tile([P, B], F32, name="largest")
+        total = keep.tile([P, B], F32, name="total")
+        for t in range(PACK):
+            j0 = 0
+            for engine, width in CHUNKS[t]:
+                picked = keep.tile([P, width], F32, name="picked%d_%d" % (t, j0))
+                window = x_sb[t][:].indirect(offsets[:, j0 // LIST_ROWS : (j0 + width) // LIST_ROWS])
+                if engine == "v":
+                    nc.vector.tensor_copy(picked[:], window)
+                else:
+                    nc.scalar.activation(picked[:], window, COPY)
+                groups = slice(j0 // GROUP, (j0 + width) // GROUP)
+                by_group = picked[:].rearrange("p (b e) -> p b e", e=GROUP)
+                nc.vector.tensor_reduce(largest[:, groups], by_group, AXIS_X, ALU.max)
+                nc.vector.tensor_reduce(total[:, groups], by_group, AXIS_X, ALU.add)
+                j0 = j0 + width
+                if j0 % (J // 2) == 0:
+                    half = slice(j0 // GROUP - B // 2, j0 // GROUP)
+                    scaler = nc.vector if (t == PACK - 1 and j0 == J) else nc.gpsimd
+                    scaler.tensor_scalar(u_bf[:, half, t], largest[:, half], fa_sb[:, t : t + 1], 0.0, ALU.mult, ALU.add)
+                    scaler.tensor_scalar(v_bf[:, half, t], total[:, half], fb_mean[:, t : t + 1], 0.0, ALU.mult, ALU.add)
+
+        u_codes = keep.tile([P, B], U32, name="u_codes", align_bytes=64)
+        v_codes = keep.tile([P, B], U32, name="v_codes", align_bytes=64)
+        u_scales = keep.tile([P, B], U8, name="u_scales", align_bytes=64)
+        v_scales = keep.tile([P, B], U8, name="v_scales", align_bytes=64)
+        nc.vector.quantize_mx(out=u_codes[:].bitcast(FP8X4), scales=u_scales[:], in_=u_bf[:].rearrange("p b t -> p (b t)"))
+        nc.vector.quantize_mx(out=v_codes[:].bitcast(FP8X4), scales=v_scales[:], in_=v_bf[:].rearrange("p b t -> p (b t)"))
+
+        for m in range(N // P):
+            nc.tensor.matmul_mx(
+                out=acc[m][:],
+                lhsT=wa_sb[:, 2 * m * P : 2 * (m + 1) * P].bitcast(FP4X4),
+                lhsT_scale=scales[:, wa_at + m * P : wa_at + (m + 1) * P],
+                rhs=u_codes[:].bitcast(FP8X4),
+                rhs_scale=u_scales[:],
+                start=False,
+                stop=False,
+            )
+        for m in range(N // P):
+            nc.tensor.matmul_mx(
+                out=acc[m][:],
+                lhsT=wb_sb[:, m * P : (m + 1) * P].bitcast(FP8X4),
+                lhsT_scale=scales[:, wb_at + m * P : wb_at + (m + 1) * P],
+                rhs=v_codes[:].bitcast(FP8X4),
+                rhs_scale=v_scales[:],
+                start=False,
+                stop=True,
+            )
+            result = keep.tile([P, B], F32, name="result%d" % m)
+            if m % 2 == 0:
+                nc.vector.tensor_copy(result[:], acc[m][:])
+            else:
+                nc.scalar.copy(result[:], acc[m][:])
+            nc.sync.dma_start(out[m * P : (m + 1) * P, :], result[:])

@@ -22,11 +22,11 @@ PACK = 4
 GROUP = 8
 LIST_ROWS = 16
 CHUNKS = (
-    (("s", 128), ("s", 384), ("s", 512)),
-    (("s", 512), ("s", 512)),
-    (("s", 512), ("s", 512)),
-    (("s", 256), ("s", 256), ("s", 256), ("s", 128), ("s", 128)),
+    (("v", 128), ("s", 256), ("s", 320), ("s", 320)),
+    (("s", 352), ("s", 352), ("s", 320)),
+    (("s", 352), ("s", 352), ("s", 320)),
 )
+LAST = (416, 832)
 
 
 def tile_list_group_range_pooling_kernel(
@@ -43,12 +43,17 @@ def tile_list_group_range_pooling_kernel(
         fa_sb = keep.tile([P, PACK], F32, name="fa_sb")
         fb_sb = keep.tile([P, PACK], F32, name="fb_sb")
         fb_mean = keep.tile([P, PACK], F32, name="fb_mean")
+        scale_rows = keep.tile([16, 3 * N + B], U8, name="scale_rows")
+        wa_at, wb_at, wc_at, gq_at = 0, N, 2 * N, 3 * N
 
         nc.sync.dma_start(x_sb[0][:], x_rows[:, 0, :])
         nc.scalar.dma_start(fb_sb[:], fb.rearrange("(p t) o -> p (t o)", t=PACK))
         nc.sync.dma_start(offsets[:], offs)
         nc.scalar.dma_start(fa_sb[:], fa.rearrange("(p t) o -> p (t o)", t=PACK))
-        for t in range(1, PACK):
+        nc.sync.dma_start(x_sb[1][:], x_rows[:, 1, :])
+        for at, src, width in ((wa_at, wa_scales, N), (wb_at, wb_scales, N), (wc_at, wc_scales, N), (gq_at, gq_scales, B)):
+            nc.sync.dma_start(scale_rows[:, at : at + width].bitcast(I32), src[0].bitcast(I32))
+        for t in range(2, PACK):
             nc.sync.dma_start(x_sb[t][:], x_rows[:, t, :])
         nc.scalar.activation(fb_mean[:], fb_sb[:], COPY, scale=1.0 / GROUP)
 
@@ -57,19 +62,19 @@ def tile_list_group_range_pooling_kernel(
         wc_sb = keep.tile([P, N], U32, name="wc_sb", align_bytes=64)
         gq_sb = keep.tile([P, 2 * B], U8, name="gq_sb", align_bytes=64)
         nc.sync.dma_start(wc_sb[:].bitcast(I32), wc_words[0].rearrange("p n t -> p (n t)").bitcast(I32))
-        nc.sync.dma_start(wa_sb[:].bitcast(I32), wa_words[0].bitcast(I32))
-        nc.sync.dma_start(wb_sb[:].bitcast(I32), wb_words[0].rearrange("p n t -> p (n t)").bitcast(I32))
         nc.sync.dma_start(gq_sb[:].bitcast(I32), gq_words[0].bitcast(I32))
-
         scales = keep.tile([P, 3 * N + B], U8, name="scales", align_bytes=64)
         nc.vector.memset(scales[:].bitcast(I32), 0)
-        wa_at, wb_at, wc_at, gq_at = 0, N, 2 * N, 3 * N
-        for at, src, width in ((wa_at, wa_scales, N), (wb_at, wb_scales, N), (wc_at, wc_scales, N), (gq_at, gq_scales, B)):
-            nc.scalar.dma_start(scales[0:16, at : at + width].bitcast(I32), src[0].bitcast(I32))
-        for q in range(1, 4):
-            nc.gpsimd.dma_start(scales[32 * q : 32 * q + 4, :].bitcast(I32), scales[4 * q : 4 * q + 4, :].bitcast(I32))
+        for q in range(4):
+            nc.sync.dma_start(scales[32 * q : 32 * q + 4, :].bitcast(I32), scale_rows[4 * q : 4 * q + 4, :].bitcast(I32))
+        nc.sync.dma_start(wa_sb[:].bitcast(I32), wa_words[0].bitcast(I32))
+        nc.sync.dma_start(wb_sb[:].bitcast(I32), wb_words[0].rearrange("p n t -> p (n t)").bitcast(I32))
 
         acc = [psum.tile([P, B], F32, name="acc%d" % m) for m in range(N // P)]
+        u_codes = keep.tile([P, B], U32, name="u_codes", align_bytes=64)
+        v_codes = keep.tile([P, B], U32, name="v_codes", align_bytes=64)
+        u_scales = keep.tile([P, B], U8, name="u_scales", align_bytes=64)
+        v_scales = keep.tile([P, B], U8, name="v_scales", align_bytes=64)
         for m in range(N // P):
             nc.tensor.matmul_mx(
                 out=acc[m][:],
@@ -81,36 +86,53 @@ def tile_list_group_range_pooling_kernel(
                 stop=False,
             )
 
-        u_bf = keep.tile([P, B, PACK], BF16, name="u_bf", align_bytes=64)
-        v_bf = keep.tile([P, B, PACK], BF16, name="v_bf", align_bytes=64)
-        largest = keep.tile([P, B], F32, name="largest")
-        total = keep.tile([P, B], F32, name="total")
-        for t in range(PACK):
+        largest = keep.tile([P, PACK, B], F32, name="largest")
+        total = keep.tile([P, PACK, B], F32, name="total")
+
+        def gather(engine, t, j0, j1):
+            picked = keep.tile([P, j1 - j0], F32, name="picked%d_%d" % (t, j0), align_bytes=64)
+            window = x_sb[t][:].indirect(offsets[:, j0 // LIST_ROWS : j1 // LIST_ROWS])
+            if engine == "v":
+                nc.vector.tensor_copy(picked[:], window)
+            else:
+                nc.scalar.activation(picked[:], window, COPY)
+            return picked[:].rearrange("p (b e) -> p b e", e=GROUP)
+
+        def pool_groups(dst, t, j0, j1, by_group, op):
+            nc.vector.tensor_reduce(dst[:, t, j0 // GROUP : j1 // GROUP], by_group, AXIS_X, op)
+
+        for t in range(PACK - 1):
             j0 = 0
             for engine, width in CHUNKS[t]:
-                picked = keep.tile([P, width], F32, name="picked%d_%d" % (t, j0))
-                window = x_sb[t][:].indirect(offsets[:, j0 // LIST_ROWS : (j0 + width) // LIST_ROWS])
-                if engine == "v":
-                    nc.vector.tensor_copy(picked[:], window)
-                else:
-                    nc.scalar.activation(picked[:], window, COPY)
-                groups = slice(j0 // GROUP, (j0 + width) // GROUP)
-                by_group = picked[:].rearrange("p (b e) -> p b e", e=GROUP)
-                nc.vector.tensor_reduce(largest[:, groups], by_group, AXIS_X, ALU.max)
-                nc.vector.tensor_reduce(total[:, groups], by_group, AXIS_X, ALU.add)
+                by_group = gather(engine, t, j0, j0 + width)
+                pool_groups(largest, t, j0, j0 + width, by_group, ALU.max)
+                pool_groups(total, t, j0, j0 + width, by_group, ALU.add)
                 j0 = j0 + width
-                if j0 % (J // 2) == 0:
-                    half = slice(j0 // GROUP - B // 2, j0 // GROUP)
-                    scaler = nc.vector if (t == PACK - 1 and j0 == J) else nc.gpsimd
-                    scaler.tensor_scalar(u_bf[:, half, t], largest[:, half], fa_sb[:, t : t + 1], 0.0, ALU.mult, ALU.add)
-                    scaler.tensor_scalar(v_bf[:, half, t], total[:, half], fb_mean[:, t : t + 1], 0.0, ALU.mult, ALU.add)
+        t = PACK - 1
+        a, b = LAST
+        first, second, third = gather("s", t, 0, a), gather("s", t, a, b), gather("s", t, b, J)
+        pool_groups(largest, t, 0, a, first, ALU.max)
+        pool_groups(total, t, 0, a, first, ALU.add)
+        rounded = keep.tile([P, 2, B, PACK], BF16, name="rounded", tag="picked3_0", align_bytes=64)
+        u_bf, v_bf = rounded[:, 0], rounded[:, 1]
+        for s in (0, 1):
+            nc.scalar.activation(u_bf[:, :, s], largest[:, s, :], COPY, scale=fa_sb[:, s : s + 1])
+        for s in (0, 1):
+            nc.scalar.activation(v_bf[:, :, s], total[:, s, :], COPY, scale=fb_mean[:, s : s + 1])
 
-        u_codes = keep.tile([P, B], U32, name="u_codes", align_bytes=64)
-        v_codes = keep.tile([P, B], U32, name="v_codes", align_bytes=64)
-        u_scales = keep.tile([P, B], U8, name="u_scales", align_bytes=64)
-        v_scales = keep.tile([P, B], U8, name="v_scales", align_bytes=64)
-        nc.vector.quantize_mx(out=u_codes[:].bitcast(FP8X4), scales=u_scales[:], in_=u_bf[:].rearrange("p b t -> p (b t)"))
-        nc.vector.quantize_mx(out=v_codes[:].bitcast(FP8X4), scales=v_scales[:], in_=v_bf[:].rearrange("p b t -> p (b t)"))
+        def scale(dst, src, factor, s):
+            nc.vector.tensor_scalar(dst[:, :, s], src[:, s, :], factor[:, s : s + 1], None, ALU.mult)
+
+        pool_groups(largest, t, a, b, second, ALU.max)
+        pool_groups(largest, t, b, J, third, ALU.max)
+        scale(u_bf, largest, fa_sb, 2)
+        pool_groups(total, t, a, b, second, ALU.add)
+        scale(u_bf, largest, fa_sb, 3)
+        pool_groups(total, t, b, J, third, ALU.add)
+        nc.vector.quantize_mx(out=u_codes[:].bitcast(FP8X4), scales=u_scales[:], in_=u_bf.rearrange("p b t -> p (b t)"))
+        scale(v_bf, total, fb_mean, 2)
+        scale(v_bf, total, fb_mean, 3)
+        nc.vector.quantize_mx(out=v_codes[:].bitcast(FP8X4), scales=v_scales[:], in_=v_bf.rearrange("p b t -> p (b t)"))
 
         for m in range(N // P):
             nc.tensor.matmul_mx(

@@ -1,6 +1,7 @@
 from contextlib import ExitStack
 
 import concourse.mybir as mybir
+from concourse.masks import make_identity
 
 K, T, J, B, N = 512, 2048, 1024, 128, 512
 FLOPS = 3 * 2 * K * N * B
@@ -21,12 +22,8 @@ P = 128
 PACK = 4
 GROUP = 8
 LIST_ROWS = 16
-CHUNKS = (
-    (("v", 128), ("s", 256), ("s", 320), ("s", 320)),
-    (("s", 352), ("s", 352), ("s", 320)),
-    (("s", 352), ("s", 352), ("s", 320)),
-)
-LAST = (416, 832)
+CUTS = (320, 704)
+LAST_CUTS = (384, 512, 832)
 
 
 def tile_list_group_range_pooling_kernel(
@@ -75,6 +72,52 @@ def tile_list_group_range_pooling_kernel(
         v_codes = keep.tile([P, B], U32, name="v_codes", align_bytes=64)
         u_scales = keep.tile([P, B], U8, name="u_scales", align_bytes=64)
         v_scales = keep.tile([P, B], U8, name="v_scales", align_bytes=64)
+        identity = keep.tile([P, P], F32, name="identity")
+        make_identity(nc, identity[:])
+        u_bf = keep.tile([P, B, PACK], BF16, name="u_bf", align_bytes=64)
+        v_bf = keep.tile([P, B, PACK], BF16, name="v_bf", align_bytes=64)
+        EARLY = PACK - 1
+        largest = keep.tile([P, PACK, B], F32, name="largest")
+        total = keep.tile([P, B], F32, name="total")
+        sums_turned = psum.tile([B, EARLY, P], F32, name="sums_turned")
+        sums_back = psum.tile([P, EARLY, B], F32, name="sums_back")
+
+        def gather(engine, dst, t, j0, j1):
+            window = x_sb[t][:].indirect(offsets[:, j0 // LIST_ROWS : j1 // LIST_ROWS])
+            if engine == "v":
+                nc.vector.tensor_copy(dst, window)
+            else:
+                nc.scalar.activation(dst, window, COPY)
+
+        def pool_groups(dst, j0, j1, src, op):
+            nc.vector.tensor_reduce(dst[:, j0 // GROUP : j1 // GROUP], src.rearrange("p (b e) -> p b e", e=GROUP), AXIS_X, op)
+
+        def scale_early(dst, src, factor):
+            nc.vector.tensor_tensor(
+                dst[:, :, :EARLY].rearrange("p (c i) t -> p c t i", i=2),
+                src.rearrange("p t (c i) -> p c t i", i=2),
+                factor[:, :EARLY].unsqueeze(1).unsqueeze(3).to_broadcast([P, B // 2, EARLY, 2]),
+                ALU.mult,
+            )
+
+        def scale_last(dst, src, factor):
+            nc.vector.tensor_scalar(dst[:, :, EARLY], src, factor[:, EARLY:], None, ALU.mult)
+
+        a, b = CUTS
+        for t in range(EARLY):
+            picked = keep.tile([P, J], F32, name="picked%d" % t)
+            gather("s", picked[:, :a], t, 0, a)
+            gather("v", picked[:, a:b], t, a, b)
+            gather("s", picked[:, b:], t, b, J)
+            for j0, j1 in ((0, a), (a, b), (b, J)):
+                pool_groups(largest[:, t, :], j0, j1, picked[:, j0:j1], ALU.max)
+            by_member = picked[:].rearrange("p (b e) -> p e b", e=GROUP)
+            for e in range(GROUP):
+                nc.tensor.matmul(
+                    sums_turned[:, t, :], by_member[:, e, :], identity[:], start=(e == 0), stop=(e == GROUP - 1), is_transpose=True
+                )
+        scale_early(u_bf, largest[:, :EARLY, :], fa_sb)
+
         for m in range(N // P):
             nc.tensor.matmul_mx(
                 out=acc[m][:],
@@ -86,53 +129,33 @@ def tile_list_group_range_pooling_kernel(
                 stop=False,
             )
 
-        largest = keep.tile([P, PACK, B], F32, name="largest")
-        total = keep.tile([P, PACK, B], F32, name="total")
 
-        def gather(engine, t, j0, j1):
-            picked = keep.tile([P, j1 - j0], F32, name="picked%d_%d" % (t, j0), align_bytes=64)
-            window = x_sb[t][:].indirect(offsets[:, j0 // LIST_ROWS : j1 // LIST_ROWS])
-            if engine == "v":
-                nc.vector.tensor_copy(picked[:], window)
-            else:
-                nc.scalar.activation(picked[:], window, COPY)
-            return picked[:].rearrange("p (b e) -> p b e", e=GROUP)
+        t = EARLY
+        a, b, c = LAST_CUTS
+        first = keep.tile([P, a], F32, name="first")
+        second = keep.tile([P, c - a], F32, name="second")
+        third = keep.tile([P, J - c], F32, name="third")
+        gather("s", first[:], t, 0, a)
+        gather("v", second[:, : b - a], t, a, b)
+        gather("s", second[:, b - a :], t, b, c)
+        gather("s", third[:], t, c, J)
+        pool_groups(largest[:, t, :], 0, a, first[:], ALU.max)
+        pool_groups(total, 0, a, first[:], ALU.add)
 
-        def pool_groups(dst, t, j0, j1, by_group, op):
-            nc.vector.tensor_reduce(dst[:, t, j0 // GROUP : j1 // GROUP], by_group, AXIS_X, op)
+        sums_sb = keep.tile([B, EARLY, P], F32, name="sums_sb", tag="first")
+        nc.scalar.copy(sums_sb[:], sums_turned[:])
+        for s in range(EARLY):
+            nc.tensor.transpose(sums_back[:, s, :], sums_sb[:, s, :], identity[:])
 
-        for t in range(PACK - 1):
-            j0 = 0
-            for engine, width in CHUNKS[t]:
-                by_group = gather(engine, t, j0, j0 + width)
-                pool_groups(largest, t, j0, j0 + width, by_group, ALU.max)
-                pool_groups(total, t, j0, j0 + width, by_group, ALU.add)
-                j0 = j0 + width
-        t = PACK - 1
-        a, b = LAST
-        first, second, third = gather("s", t, 0, a), gather("s", t, a, b), gather("s", t, b, J)
-        pool_groups(largest, t, 0, a, first, ALU.max)
-        pool_groups(total, t, 0, a, first, ALU.add)
-        rounded = keep.tile([P, 2, B, PACK], BF16, name="rounded", tag="picked3_0", align_bytes=64)
-        u_bf, v_bf = rounded[:, 0], rounded[:, 1]
-        for s in (0, 1):
-            nc.scalar.activation(u_bf[:, :, s], largest[:, s, :], COPY, scale=fa_sb[:, s : s + 1])
-        for s in (0, 1):
-            nc.scalar.activation(v_bf[:, :, s], total[:, s, :], COPY, scale=fb_mean[:, s : s + 1])
-
-        def scale(dst, src, factor, s):
-            nc.vector.tensor_scalar(dst[:, :, s], src[:, s, :], factor[:, s : s + 1], None, ALU.mult)
-
-        pool_groups(largest, t, a, b, second, ALU.max)
-        pool_groups(largest, t, b, J, third, ALU.max)
-        scale(u_bf, largest, fa_sb, 2)
-        pool_groups(total, t, a, b, second, ALU.add)
-        scale(u_bf, largest, fa_sb, 3)
-        pool_groups(total, t, b, J, third, ALU.add)
-        nc.vector.quantize_mx(out=u_codes[:].bitcast(FP8X4), scales=u_scales[:], in_=u_bf.rearrange("p b t -> p (b t)"))
-        scale(v_bf, total, fb_mean, 2)
-        scale(v_bf, total, fb_mean, 3)
-        nc.vector.quantize_mx(out=v_codes[:].bitcast(FP8X4), scales=v_scales[:], in_=v_bf.rearrange("p b t -> p (b t)"))
+        pool_groups(largest[:, t, :], a, c, second[:], ALU.max)
+        pool_groups(largest[:, t, :], c, J, third[:], ALU.max)
+        pool_groups(total, a, c, second[:], ALU.add)
+        scale_last(u_bf, largest[:, t, :], fa_sb)
+        pool_groups(total, c, J, third[:], ALU.add)
+        nc.vector.quantize_mx(out=u_codes[:].bitcast(FP8X4), scales=u_scales[:], in_=u_bf[:].rearrange("p b t -> p (b t)"))
+        scale_last(v_bf, total[:], fb_mean)
+        scale_early(v_bf, sums_back[:], fb_mean)
+        nc.vector.quantize_mx(out=v_codes[:].bitcast(FP8X4), scales=v_scales[:], in_=v_bf[:].rearrange("p b t -> p (b t)"))
 
         for m in range(N // P):
             nc.tensor.matmul_mx(

@@ -23,7 +23,7 @@ PACK = 4
 GROUP = 8
 LIST_ROWS = 16
 CUTS = (320, 704)
-LAST_CUTS = (384, 512, 832)
+LAST_CUTS = (320, 448, 800)
 
 
 def tile_list_group_range_pooling_kernel(
@@ -150,7 +150,7 @@ def tile_list_group_range_pooling_kernel(
         pool_groups(largest[:, t, :], a, c, second[:], ALU.max)
         pool_groups(largest[:, t, :], c, J, third[:], ALU.max)
         pool_groups(total, a, c, second[:], ALU.add)
-        scale_last(u_bf, largest[:, t, :], fa_sb)
+        nc.scalar.activation(u_bf[:, :, t], largest[:, t, :], COPY, scale=fa_sb[:, t:])
         pool_groups(total, c, J, third[:], ALU.add)
         nc.vector.quantize_mx(out=u_codes[:].bitcast(FP8X4), scales=u_scales[:], in_=u_bf[:].rearrange("p b t -> p (b t)"))
         scale_last(v_bf, total[:], fb_mean)

from contextlib import ExitStack

import concourse.mybir as mybir
from concourse.masks import make_identity

K, T, J, B, N = 512, 2048, 1024, 128, 512
FLOPS = 3 * 2 * K * N * B

F32 = mybir.dt.float32
BF16 = mybir.dt.bfloat16
I32 = mybir.dt.int32
U32 = mybir.dt.uint32
U16 = mybir.dt.uint16
U8 = mybir.dt.uint8
FP8X4 = mybir.dt.float8_e4m3fn_x4
FP4X4 = mybir.dt.float4_e2m1fn_x4
ALU = mybir.AluOpType
COPY = mybir.ActivationFunctionType.Copy
AXIS_X = mybir.AxisListType.X

P = 128
PACK = 4
GROUP = 8
LIST_ROWS = 16
CUTS = (320, 704)
LAST_CUTS = (320, 448, 800)


def tile_list_group_range_pooling_kernel(
    tc, xt, fa, fb, wa_words, wa_scales, wb_words, wb_scales, gq_words, gq_scales, wc_words, wc_scales, offs, out
):
    nc = tc.nc
    with ExitStack() as ctx:
        keep = ctx.enter_context(tc.tile_pool(name="keep", bufs=1))
        psum = ctx.enter_context(tc.psum_pool(name="psum", bufs=1))

        x_rows = xt.rearrange("(p t) c -> p t c", t=PACK)
        x_sb = [keep.tile([P, T], F32, name="x%d" % t) for t in range(PACK)]
        offsets = keep.tile([P, J // LIST_ROWS], U16, name="offsets")
        fa_sb = keep.tile([P, PACK], F32, name="fa_sb")
        fb_sb = keep.tile([P, PACK], F32, name="fb_sb")
        fb_mean = keep.tile([P, PACK], F32, name="fb_mean")
        scale_rows = keep.tile([16, 3 * N + B], U8, name="scale_rows")
        wa_at, wb_at, wc_at, gq_at = 0, N, 2 * N, 3 * N

        nc.sync.dma_start(x_sb[0][:], x_rows[:, 0, :])
        nc.scalar.dma_start(fb_sb[:], fb.rearrange("(p t) o -> p (t o)", t=PACK))
        nc.sync.dma_start(offsets[:], offs)
        nc.scalar.dma_start(fa_sb[:], fa.rearrange("(p t) o -> p (t o)", t=PACK))
        nc.sync.dma_start(x_sb[1][:], x_rows[:, 1, :])
        for at, src, width in ((wa_at, wa_scales, N), (wb_at, wb_scales, N), (wc_at, wc_scales, N), (gq_at, gq_scales, B)):
            nc.sync.dma_start(scale_rows[:, at : at + width].bitcast(I32), src[0].bitcast(I32))
        for t in range(2, PACK):
            nc.sync.dma_start(x_sb[t][:], x_rows[:, t, :])
        nc.scalar.activation(fb_mean[:], fb_sb[:], COPY, scale=1.0 / GROUP)

        wa_sb = keep.tile([P, 2 * N], U8, name="wa_sb", align_bytes=64)
        wb_sb = keep.tile([P, N], U32, name="wb_sb", align_bytes=64)
        wc_sb = keep.tile([P, N], U32, name="wc_sb", align_bytes=64)
        gq_sb = keep.tile([P, 2 * B], U8, name="gq_sb", align_bytes=64)
        nc.sync.dma_start(wc_sb[:].bitcast(I32), wc_words[0].rearrange("p n t -> p (n t)").bitcast(I32))
        nc.sync.dma_start(gq_sb[:].bitcast(I32), gq_words[0].bitcast(I32))
        scales = keep.tile([P, 3 * N + B], U8, name="scales", align_bytes=64)
        nc.vector.memset(scales[:].bitcast(I32), 0)
        for q in range(4):
            nc.sync.dma_start(scales[32 * q : 32 * q + 4, :].bitcast(I32), scale_rows[4 * q : 4 * q + 4, :].bitcast(I32))
        nc.sync.dma_start(wa_sb[:].bitcast(I32), wa_words[0].bitcast(I32))
        nc.sync.dma_start(wb_sb[:].bitcast(I32), wb_words[0].rearrange("p n t -> p (n t)").bitcast(I32))

        acc = [psum.tile([P, B], F32, name="acc%d" % m) for m in range(N // P)]
        u_codes = keep.tile([P, B], U32, name="u_codes", align_bytes=64)
        v_codes = keep.tile([P, B], U32, name="v_codes", align_bytes=64)
        u_scales = keep.tile([P, B], U8, name="u_scales", align_bytes=64)
        v_scales = keep.tile([P, B], U8, name="v_scales", align_bytes=64)
        identity = keep.tile([P, P], F32, name="identity")
        make_identity(nc, identity[:])
        u_bf = keep.tile([P, B, PACK], BF16, name="u_bf", align_bytes=64)
        v_bf = keep.tile([P, B, PACK], BF16, name="v_bf", align_bytes=64)
        EARLY = PACK - 1
        largest = keep.tile([P, PACK, B], F32, name="largest")
        total = keep.tile([P, B], F32, name="total")
        sums_turned = psum.tile([B, EARLY, P], F32, name="sums_turned")
        sums_back = psum.tile([P, EARLY, B], F32, name="sums_back")

        def gather(engine, dst, t, j0, j1):
            window = x_sb[t][:].indirect(offsets[:, j0 // LIST_ROWS : j1 // LIST_ROWS])
            if engine == "v":
                nc.vector.tensor_copy(dst, window)
            else:
                nc.scalar.activation(dst, window, COPY)

        def pool_groups(dst, j0, j1, src, op):
            nc.vector.tensor_reduce(dst[:, j0 // GROUP : j1 // GROUP], src.rearrange("p (b e) -> p b e", e=GROUP), AXIS_X, op)

        def scale_early(dst, src, factor):
            nc.vector.tensor_tensor(
                dst[:, :, :EARLY].rearrange("p (c i) t -> p c t i", i=2),
                src.rearrange("p t (c i) -> p c t i", i=2),
                factor[:, :EARLY].unsqueeze(1).unsqueeze(3).to_broadcast([P, B // 2, EARLY, 2]),
                ALU.mult,
            )

        def scale_last(dst, src, factor):
            nc.vector.tensor_scalar(dst[:, :, EARLY], src, factor[:, EARLY:], None, ALU.mult)

        a, b = CUTS
        for t in range(EARLY):
            picked = keep.tile([P, J], F32, name="picked%d" % t)
            gather("s", picked[:, :a], t, 0, a)
            gather("v", picked[:, a:b], t, a, b)
            gather("s", picked[:, b:], t, b, J)
            for j0, j1 in ((0, a), (a, b), (b, J)):
                pool_groups(largest[:, t, :], j0, j1, picked[:, j0:j1], ALU.max)
            by_member = picked[:].rearrange("p (b e) -> p e b", e=GROUP)
            for e in range(GROUP):
                nc.tensor.matmul(
                    sums_turned[:, t, :], by_member[:, e, :], identity[:], start=(e == 0), stop=(e == GROUP - 1), is_transpose=True
                )
        scale_early(u_bf, largest[:, :EARLY, :], fa_sb)

        for m in range(N // P):
            nc.tensor.matmul_mx(
                out=acc[m][:],
                lhsT=wc_sb[:, m * P : (m + 1) * P].bitcast(FP8X4),
                lhsT_scale=scales[:, wc_at + m * P : wc_at + (m + 1) * P],
                rhs=gq_sb[:].bitcast(FP4X4),
                rhs_scale=scales[:, gq_at : gq_at + B],
                start=True,
                stop=False,
            )


        t = EARLY
        a, b, c = LAST_CUTS
        first = keep.tile([P, a], F32, name="first")
        second = keep.tile([P, c - a], F32, name="second")
        third = keep.tile([P, J - c], F32, name="third")
        gather("s", first[:], t, 0, a)
        gather("v", second[:, : b - a], t, a, b)
        gather("s", second[:, b - a :], t, b, c)
        gather("s", third[:], t, c, J)
        pool_groups(largest[:, t, :], 0, a, first[:], ALU.max)
        pool_groups(total, 0, a, first[:], ALU.add)

        sums_sb = keep.tile([B, EARLY, P], F32, name="sums_sb", tag="first")
        nc.scalar.copy(sums_sb[:], sums_turned[:])
        for s in range(EARLY):
            nc.tensor.transpose(sums_back[:, s, :], sums_sb[:, s, :], identity[:])

        pool_groups(largest[:, t, :], a, c, second[:], ALU.max)
        pool_groups(largest[:, t, :], c, J, third[:], ALU.max)
        pool_groups(total, a, c, second[:], ALU.add)
        nc.scalar.activation(u_bf[:, :, t], largest[:, t, :], COPY, scale=fa_sb[:, t:])
        pool_groups(total, c, J, third[:], ALU.add)
        nc.vector.quantize_mx(out=u_codes[:].bitcast(FP8X4), scales=u_scales[:], in_=u_bf[:].rearrange("p b t -> p (b t)"))
        scale_last(v_bf, total[:], fb_mean)
        scale_early(v_bf, sums_back[:], fb_mean)
        nc.vector.quantize_mx(out=v_codes[:].bitcast(FP8X4), scales=v_scales[:], in_=v_bf[:].rearrange("p b t -> p (b t)"))

        for m in range(N // P):
            nc.tensor.matmul_mx(
                out=acc[m][:],
                lhsT=wa_sb[:, 2 * m * P : 2 * (m + 1) * P].bitcast(FP4X4),
                lhsT_scale=scales[:, wa_at + m * P : wa_at + (m + 1) * P],
                rhs=u_codes[:].bitcast(FP8X4),
                rhs_scale=u_scales[:],
                start=False,
                stop=False,
            )
        for m in range(N // P):
            nc.tensor.matmul_mx(
                out=acc[m][:],
                lhsT=wb_sb[:, m * P : (m + 1) * P].bitcast(FP8X4),
                lhsT_scale=scales[:, wb_at + m * P : wb_at + (m + 1) * P],
                rhs=v_codes[:].bitcast(FP8X4),
                rhs_scale=v_scales[:],
                start=False,
                stop=True,
            )
            result = keep.tile([P, B], F32, name="result%d" % m)
            if m % 2 == 0:
                nc.vector.tensor_copy(result[:], acc[m][:])
            else:
                nc.scalar.copy(result[:], acc[m][:])
            nc.sync.dma_start(out[m * P : (m + 1) * P, :], result[:])
